import numpy as np
import ml_dtypes


def mxq(x, axis, fmt="e4m3"):
    dtype, down = {"e4m3": (ml_dtypes.float8_e4m3fn, 7), "e5m2": (ml_dtypes.float8_e5m2, 14)}[fmt]
    v = np.moveaxis(np.asarray(x, np.float32).astype(ml_dtypes.bfloat16).astype(np.float64), axis, -1)
    blocks = v.reshape(v.shape[:-1] + (-1, 32))
    amax = np.abs(blocks).max(-1, keepdims=True)
    byte = np.maximum(np.where(amax > 0, np.frexp(amax)[1] - 1 + 127, 0) - down, 1)
    scale = np.exp2(byte - 127.0)
    codes = (blocks / scale).astype(np.float32).astype(dtype).astype(np.float64)
    return np.moveaxis((codes * scale).reshape(v.shape), -1, axis)


WIDE = False


def mx_kscale(k):
    if not WIDE:
        return np.ones(k)
    levels = np.array([10, -10, 5, -5, 0])
    if k % 512:
        return np.exp2(np.random.permutation(np.resize(levels, k // 32))).repeat(32)
    a = np.empty((k // 512, 16))
    for p in range(k // 512):
        a[p, :8] = np.random.permutation(np.resize(levels, 8))
        for g in range(8):
            far = levels[np.abs(levels - a[p, g]) >= 10]
            a[p, g + 8] = far[np.random.randint(len(far))]
    return np.exp2(a.ravel()).repeat(32)


def f64(x):
    return np.asarray(x).astype(np.float64)


def striped(idx):
    return np.tile(idx.reshape(-1, 16).T, (8, 1)).astype(np.uint16)


def unstriped(offs):
    return offs[:16].T.reshape(-1).astype(np.int64)


E2M1 = np.array([0.0, 0.5, 1.0, 1.5, 2.0, 3.0, 4.0, 6.0, -0.0, -0.5, -1.0, -1.5, -2.0, -3.0, -4.0, -6.0])


def pack_weight(w, fmt):
    k, n = w.shape
    w = f64(np.asarray(w, np.float32).astype(ml_dtypes.bfloat16)).reshape(k // 32, 32, n)
    amax = np.abs(w).max(1)
    if fmt == "e4m3":
        byte = np.frexp(amax)[1] - 1 + 127 - 7
    else:
        mant, ex = np.frexp(amax / 6.0)
        byte = np.where(mant > 0.5, ex, ex - 1) + 127
    byte = np.clip(np.where(amax > 0, byte, 1), 1, 254)
    scaled = (w * np.exp2(127.0 - byte)[:, None, :]).reshape(k, n).astype(np.float32)
    by_word = np.ascontiguousarray(scaled.reshape(k // 512, 128, 4, n).transpose(0, 1, 3, 2))
    if fmt == "e4m3":
        words = by_word.astype(ml_dtypes.float8_e4m3fn).view(np.uint8)
    else:
        c = by_word.astype(ml_dtypes.float4_e2m1fn).view(np.uint8) & 0xF
        words = (c[..., 0::2] | (c[..., 1::2] << 4)).reshape(k // 512, 128, 2 * n)
    return np.ascontiguousarray(words), np.ascontiguousarray(byte.astype(np.uint8).reshape(k // 512, 16, n))


def unpack_weight(words, scales, fmt):
    g, _, n = scales.shape
    words = np.ascontiguousarray(words).reshape(g, 128, n, -1)
    if fmt == "e4m3":
        vals = words.view(ml_dtypes.float8_e4m3fn).astype(np.float64)
    else:
        nib = np.empty((g, 128, n, 4), np.uint8)
        nib[..., 0::2] = words & 0xF
        nib[..., 1::2] = words >> 4
        vals = E2M1[nib]
    vals = vals * np.repeat(np.exp2(scales.astype(np.float64) - 127.0), 8, axis=1)[..., None]
    return vals.transpose(0, 1, 3, 2).reshape(g * 512, n)


def gelu(v):
    return 0.5 * v * (1.0 + np.tanh(np.sqrt(2.0 / np.pi) * (v + 0.044715 * v**3)))


T, S, K, H, N, T2 = 2048, 512, 512, 1024, 768, 1024

def setup_inputs():
    n = np.random.standard_normal
    s = mx_kscale(K)[:, None]
    u = mx_kscale(H)[:, None]
    tab_words, tab_scales = pack_weight(n((K, T)) * s, "e4m3")
    tab2_words, tab2_scales = pack_weight(n((K, T)) * s, "e4m3")
    w2_words, w2_scales = pack_weight(0.7 * n((K, H)) / np.sqrt(K) / s, "e2m1")
    w3_words, w3_scales = pack_weight(n((K, H)) / np.sqrt(K) / s, "e4m3")
    perm = np.random.permutation(T2)
    return {
        "tab_words": tab_words, "tab_scales": tab_scales,
        "tab2_words": tab2_words, "tab2_scales": tab2_scales,
        "offs": striped(np.random.permutation(T)[:S]),
        "offs2": striped(np.random.permutation(T)[:S]),
        "offs3": striped(perm[:S]), "offs4": striped(perm[S:]),
        "w1": (n((K, H)) / np.sqrt(K) / s).astype(np.float32),
        "w2_words": w2_words, "w2_scales": w2_scales,
        "w3_words": w3_words, "w3_scales": w3_scales,
        "w4": (n((K, H)) / np.sqrt(K) / s).astype(np.float32),
        "audio": (n((K, S)) * s).astype(np.float32),
        "wg1": np.exp(0.3 * n((128, S))).astype(np.float32),
        "wg2": np.exp(0.3 * n((128, S))).astype(np.float32),
        "gain": (np.exp(0.2 * n(H)) * u[:, 0]).astype(np.float32),
        "bias": (0.4 * n(H) * u[:, 0]).astype(np.float32),
        "w5": (n((H, N)) / np.sqrt(H) / u).astype(np.float32),
        "rest": (0.4 * n(N)).astype(np.float32)}

def reference(tab_words, tab_scales, tab2_words, tab2_scales, offs, offs2, offs3, offs4, w1, w2_words, w2_scales, w3_words, w3_scales, w4, audio, wg1, wg2, gain, bias, w5, rest):
    v = unpack_weight(tab_words, tab_scales, "e4m3")[:, unstriped(offs)]
    v2 = unpack_weight(tab2_words, tab2_scales, "e4m3")[:, unstriped(offs2)]
    a = mxq(f64(w1), 0, "e4m3").T @ v
    b = unpack_weight(w2_words, w2_scales, "e2m1").T @ v
    h1 = 0.5 * a * (1 + np.tanh(np.sqrt(2 / np.pi) * (a + 0.044715 * a ** 3))) + b
    e = unpack_weight(w3_words, w3_scales, "e4m3").T @ v2 + mxq(f64(w4), 0, "e4m3").T @ mxq(f64(audio), 0, "e4m3")
    h2 = 0.5 * e * (1 + np.tanh(np.sqrt(2 / np.pi) * (e + 0.044715 * e ** 3)))
    page = np.zeros((H, T2))
    page[:, unstriped(offs3)] = np.tile(f64(wg1), (H // 128, 1)) * h1
    page[:, unstriped(offs4)] = np.tile(f64(wg2), (H // 128, 1)) * h2
    x = page * f64(gain)[:, None] + f64(bias)[:, None]
    y = mxq(f64(w5), 0, "e4m3").T @ mxq(x, 0, "e4m3")
    return y + f64(rest)[:, None]

@@ -1,0 +1,308 @@
+from contextlib import ExitStack
+
+import concourse.mybir as mybir
+
+T, S, K, H, N, T2 = 2048, 512, 512, 1024, 768, 1024
+FLOPS = 2 * (4 * K * H * S + H * N * T2)
+
+F32 = mybir.dt.float32
+BF16 = mybir.dt.bfloat16
+I32 = mybir.dt.int32
+U32 = mybir.dt.uint32
+U16 = mybir.dt.uint16
+U8 = mybir.dt.uint8
+FP8X4 = mybir.dt.float8_e4m3fn_x4
+FP4X4 = mybir.dt.float4_e2m1fn_x4
+ACT = mybir.ActivationFunctionType
+ALU = mybir.AluOpType
+
+P = 128
+PACK = 4
+PASSES = H // (P * PACK)
+SLICES = PASSES * PACK
+BANK = 512
+HALVES = T2 // BANK
+N_TILES = N // P
+W5_PIECE = N // 2
+
+
+def tile_list_blendshape_rig_weave_kernel(
+    tc, tab_words, tab_scales, tab2_words, tab2_scales, offs, offs2, offs3, offs4, w1, w2_words, w2_scales,
+    w3_words, w3_scales, w4, audio, wg1, wg2, gain, bias, w5, rest, out,
+):
+    nc = tc.nc
+    with ExitStack() as ctx:
+        lists = ctx.enter_context(tc.tile_pool(name="lists", bufs=1))
+        pool = ctx.enter_context(tc.tile_pool(name="pool", bufs=1))
+        psum = ctx.enter_context(tc.psum_pool(name="psum", bufs=1))
+
+        def sb(name, shape, dtype, tag=None):
+            return pool.tile(shape, dtype, name=name, tag=tag or name, align_bytes=64)
+
+        def bank(name, index):
+            return psum.tile([P, BANK], F32, name=name, tag="bank%d" % index)
+
+        def load_list(name, src):
+            tile = lists.tile([P, S // 16], U16, name=name)
+            nc.sync.dma_start(tile[:], src)
+            return tile
+
+        def load_bytes(name, src, width, dtype):
+            tile = sb(name, [P, width], dtype)
+            nc.sync.dma_start(tile[:].bitcast(I32), src.bitcast(I32))
+            return tile
+
+        def load_scales(name, src, width, clear, queue):
+            tile = sb(name, [P, width], U8)
+            clear.memset(tile[:].bitcast(I32), 0)
+            for q in range(4):
+                queue.dma_start(tile[32 * q : 32 * q + 4, :].bitcast(I32), src[0, 4 * q : 4 * q + 4, :].bitcast(I32))
+            return tile
+
+        def load_rows(name, src, tag=None):
+            tile = sb(name, [P, PACK, src.shape[1]], F32, tag)
+            nc.sync.dma_start(tile[:], src.rearrange("(p j) c -> p j c", j=PACK))
+            return tile
+
+        def load_gates(name, src, t0, t1, tag=None):
+            tile = sb(name, [P, t1 - t0, S], F32, tag)
+            rows = src.rearrange("(q t) j -> q t j", t=PACK)[:, t0:t1, :]
+            for quadrant in (0, 2, 1, 3):
+                nc.sync.dma_start(tile[32 * quadrant : 32 * quadrant + 32, :, :], rows)
+            return tile
+
+        def gather(name, words, scales, offsets):
+            codes = sb(name + "_codes", [P, S], U32)
+            plane = sb(name + "_plane", [P, S], U8)
+            nc.vector.tensor_copy(codes[:], words[:].bitcast(U32).indirect(offsets[:]))
+            nc.vector.tensor_copy(plane[:], scales[:].indirect(offsets[:]))
+            return codes, plane
+
+        def reorder(name, raw, dtype):
+            moved = sb(name, list(raw.shape), raw.dtype)
+            nc.vector.tensor_copy(
+                moved[:].bitcast(dtype).rearrange("p (b t m) -> p b m t", b=PASSES, t=PACK),
+                raw[:].bitcast(dtype).rearrange("p (b m t) -> p b m t", b=PASSES, t=PACK),
+            )
+            return moved
+
+        def cast_reordered(copy, stage, raw, t0, t1):
+            copy(
+                stage[:].rearrange("p (t m j) -> p m j t", t=PACK, j=PACK)[:, :, :, t0:t1],
+                raw[:].rearrange("p j (m t) -> p m j t", t=PACK)[:, :, :, t0:t1],
+            )
+
+        def cast_plain(stage, raw):
+            nc.scalar.copy(
+                stage.rearrange("p (c i j) -> p c j i", i=4, j=PACK),
+                raw[:].rearrange("p j (c i) -> p c j i", i=4),
+            )
+
+        def quantize(operand, stage, c0, c1):
+            codes, plane = operand
+            nc.vector.quantize_mx(
+                out=codes[:, c0:c1].bitcast(FP8X4), scales=plane[:, c0:c1], in_=stage[:, PACK * c0 : PACK * c1]
+            )
+
+        def mx_operand(name, width):
+            return sb(name + "_codes", [P, width], U32), sb(name + "_plane", [P, width], U8)
+
+        def matmul(acc, lhs_codes, lhs_plane, rhs, start, stop):
+            nc.tensor.matmul_mx(
+                out=acc[:], lhsT=lhs_codes, lhsT_scale=lhs_plane, rhs=rhs[0][:].bitcast(FP8X4), rhs_scale=rhs[1][:],
+                start=start, stop=stop,
+            )
+
+        def matmul8(acc, lhs, c0, rhs, start, stop):
+            matmul(acc, lhs[0][:, c0 : c0 + P].bitcast(FP8X4), lhs[1][:, c0 : c0 + P], rhs, start, stop)
+
+        idx1 = load_list("idx1", offs)
+        tab1 = load_bytes("tab1", tab_words[0].rearrange("p t i -> p (t i)"), T, I32)
+        tab1_scales = load_scales("tab1_scales", tab_scales, T, nc.vector, nc.scalar)
+        w1_raw = [load_rows("w1_raw0", w1[:, 0:BANK])]
+        w2_raw = load_bytes("w2_raw", w2_words[0], 2 * H, U8)
+        w2_scales_raw = load_scales("w2_scales_raw", w2_scales, H, nc.vector, nc.gpsimd)
+        idx3 = load_list("idx3", offs3)
+        gates1_first = load_gates("gates1_first", wg1, 0, 1)
+        gates1_rest = load_gates("gates1_rest", wg1, 1, PACK)
+        w1_raw.append(load_rows("w1_raw1", w1[:, BANK:H]))
+        audio_raw = load_rows("audio_raw", audio)
+        w4_raw = [load_rows("w4_raw%d" % b, w4[:, BANK * b : BANK * (b + 1)]) for b in range(PASSES)]
+        idx2 = load_list("idx2", offs2)
+        tab2 = load_bytes("tab2", tab2_words[0].rearrange("p t i -> p (t i)"), T, I32)
+        tab2_scales_raw = load_scales("tab2_scales", tab2_scales, T, nc.vector, nc.gpsimd)
+        w3_raw = load_bytes("w3_raw", w3_words[0].rearrange("p c i -> p (c i)"), H, I32)
+        w3_scales_raw = load_scales("w3_scales_raw", w3_scales, H, nc.vector, nc.gpsimd)
+
+        v1 = gather("v1", tab1, tab1_scales, idx1)
+        w1_mx = [mx_operand("w1_%d" % b, BANK) for b in range(PASSES)]
+        w1_stage0 = sb("w1_stage0", [P, PACK * BANK], BF16, "tab1_scales")
+        cast_reordered(nc.vector.tensor_copy, w1_stage0, w1_raw[0], 0, 1)
+        w2_codes = reorder("w2_codes", w2_raw, U16)
+        quantize(w1_mx[0], w1_stage0, 0, P)
+        w2_plane = reorder("w2_plane", w2_scales_raw, U8)
+        cast_reordered(nc.vector.tensor_copy, w1_stage0, w1_raw[0], 1, PACK)
+
+        slot_of = [0, 1, 2, 3, 1, 2, 3, 0]
+        h1 = {}
+        h2 = {}
+        pages = {}
+
+        held = {}
+
+        def mouth_products(s, gelu_tag):
+            b, t = s // PACK, slot_of[s]
+            acc_a = bank("a%d" % s, 4)
+            acc_b = bank("b%d" % s, [5, 6, 0, 1, 2, 3, 5, 6][s])
+            matmul8(acc_a, w1_mx[b], P * t, v1, True, True)
+            c0 = BANK * b + P * t
+            matmul(acc_b, w2_codes[:, 2 * c0 : 2 * c0 + 2 * P].bitcast(FP4X4), w2_plane[:, c0 : c0 + P], v1, True, True)
+            act = sb("act%d" % s, [P, S], F32, gelu_tag)
+            nc.scalar.activation(act[:], acc_a[:], ACT.Gelu_apprx_tanh)
+            held[s] = (act, acc_b)
+
+        def mouth_sum(s, h_tag):
+            act, acc_b = held[s]
+            h1[s] = sb("h1_%d" % s, [P, S], F32, h_tag)
+            nc.vector.tensor_tensor(h1[s][:], acc_b[:], act[:], ALU.add)
+
+        def mouth(s, gelu_tag, h_tag):
+            mouth_products(s, gelu_tag)
+            mouth_sum(s, h_tag)
+
+        def put_mouth(s):
+            t = slot_of[s]
+            gate = gates1_first[:, 0, :] if t == 0 else gates1_rest[:, t - 1, :]
+            pages[s] = sb("page%d" % s, [P, T2], F32)
+            nc.vector.tensor_tensor(pages[s][:].indirect(idx3[:]), h1[s][:], gate, ALU.mult)
+
+        mouth(0, "act0", "h0")
+        quantize(w1_mx[0], w1_stage0, P, 2 * P)
+        quantize(w1_mx[0], w1_stage0, 2 * P, BANK)
+        put_mouth(0)
+        mouth(1, "act1", "h1")
+        mouth(2, "page1", "h2")
+        put_mouth(1)
+        w1_stage1 = sb("w1_stage1", [P, PACK * BANK], BF16)
+        cast_reordered(nc.scalar.copy, w1_stage1, w1_raw[1], 0, PACK)
+        quantize(w1_mx[1], w1_stage1, 0, BANK)
+        mouth(3, "page2", "w1_stage1")
+        put_mouth(2)
+        audio_mx = mx_operand("audio", S)
+        audio_stage = sb("audio_stage", [P, PACK * S], BF16, "tab1_scales")
+        cast_plain(audio_stage[:], audio_raw)
+        quantize(audio_mx, audio_stage, 0, S)
+        w4_mx = [mx_operand("w4_%d" % b, BANK) for b in range(PASSES)]
+        for b in range(PASSES):
+            stage = sb("w4_stage%d" % b, [P, PACK * BANK], BF16)
+            cast_reordered(nc.scalar.copy, stage, w4_raw[b], 0, PACK)
+            quantize(w4_mx[b], stage, 0, BANK)
+        v2 = gather("v2", tab2, tab2_scales_raw, idx2)
+        w3_plane = reorder("w3_plane", w3_scales_raw, U8)
+        w3_codes = reorder("w3_codes", w3_raw, I32)
+        mouth(4, "page3", "w3_raw")
+        put_mouth(3)
+        mouth(5, "page4", "h0")
+        put_mouth(4)
+
+        w5_raw = {}
+        free_tags = ["tab1", "w1_raw0", "w1_raw1", None]
+        for b in range(PASSES):
+            for u in range(2):
+                src = w5[BANK * b : BANK * (b + 1), W5_PIECE * u : W5_PIECE * (u + 1)]
+                w5_raw[b, u] = load_rows("w5_raw%d%d" % (b, u), src, free_tags[2 * b + u])
+        gain_sb = sb("gain_sb", [P, PASSES, PACK], F32)
+        bias_sb = sb("bias_sb", [P, PASSES, PACK], F32)
+        nc.sync.dma_start(gain_sb[:], gain.rearrange("(b p t) -> p b t", b=PASSES, t=PACK))
+        nc.sync.dma_start(bias_sb[:], bias.rearrange("(b p t) -> p b t", b=PASSES, t=PACK))
+        idx4 = load_list("idx4", offs4)
+        gates2 = load_gates("gates2", wg2, 0, PACK, "w4_raw1")
+        rest_sb = sb("rest_sb", [P, N_TILES], F32)
+        with nc.allow_non_contiguous_dma(reason="one value of rest for each partition and tile"):
+            nc.sync.dma_start(rest_sb[:], rest.rearrange("(c p) -> p c", p=P))
+
+        mouth(6, "page5", "h1")
+        put_mouth(5)
+        put_mouth(6)
+
+        def brow(s):
+            b, t = s // PACK, slot_of[s]
+            acc = bank("e%d" % s, 7 * (s % 2))
+            matmul8(acc, (w3_codes, w3_plane), BANK * b + P * t, v2, True, False)
+            matmul8(acc, w4_mx[b], P * t, audio_mx, False, True)
+            h2[s] = sb("h2_%d" % s, [P, S], F32)
+            nc.scalar.activation(h2[s][:], acc[:], ACT.Gelu_apprx_tanh)
+
+        w5_mx = [mx_operand("w5_%d" % b, N) for b in range(PASSES)]
+        for b in range(PASSES):
+            stage = sb("w5_stage%d" % b, [P, PACK * N], BF16)
+            for u in range(2):
+                cast_plain(stage[:, PACK * W5_PIECE * u : PACK * W5_PIECE * (u + 1)], w5_raw[b, u])
+            quantize(w5_mx[b], stage, 0, BANK)
+            quantize(w5_mx[b], stage, BANK, N)
+
+        for s in range(SLICES):
+            brow(s)
+
+        x_tags = ["tab1_scales", "w4_stage0", None, None]
+        x_stage = {}
+        x_mx = {}
+        for b in range(PASSES):
+            for half in range(HALVES):
+                x_stage[b, half] = sb("x_stage%d%d" % (b, half), [P, PACK * BANK], BF16, x_tags[2 * b + half])
+                x_mx[b, half] = mx_operand("x%d%d" % (b, half), BANK)
+
+        def put_brow(s):
+            nc.vector.tensor_tensor(pages[s][:].indirect(idx4[:]), h2[s][:], gates2[:, slot_of[s], :], ALU.mult)
+
+        def affine(s, half, on_vector):
+            b, t = s // PACK, slot_of[s]
+            dst = x_stage[b, half][:].rearrange("p (m t) -> p m t", t=PACK)[:, :, t]
+            src = pages[s][:, BANK * half : BANK * (half + 1)]
+            g, c = gain_sb[:, b, t : t + 1], bias_sb[:, b, t : t + 1]
+            if on_vector:
+                nc.vector.tensor_scalar(dst, src, g, c, ALU.mult, ALU.add)
+            else:
+                nc.scalar.activation(dst, src, ACT.Identity, bias=c, scale=g)
+
+        groups = [(half, c) for half in range(HALVES) for c in range(N_TILES)]
+        accs = {}
+
+        def out_pass(g, b):
+            half, c = groups[g]
+            if b == 0:
+                accs[g] = bank("y%d" % g, g % 8)
+            matmul8(accs[g], w5_mx[b], P * c, x_mx[b, half], b == 0, b == PASSES - 1)
+
+        last = SLICES - 1
+        for s in range(last):
+            if s == last - 1:
+                mouth_sum(last, "h2_%d" % (last - 2))
+            put_brow(s)
+            if s == last - 2:
+                mouth_products(last, "page%d" % PACK)
+            for half in range(HALVES):
+                affine(s, half, False)
+            if s == PACK - 1:
+                for half in range(HALVES):
+                    quantize(x_mx[0, half], x_stage[0, half], 0, BANK)
+        for g in range(8):
+            out_pass(g, 0)
+        put_mouth(last)
+        put_brow(last)
+        affine(last, 0, True)
+        affine(last, 1, False)
+        for half in range(HALVES):
+            quantize(x_mx[1, half], x_stage[1, half], 0, BANK)
+
+        for g in range(len(groups)):
+            half, c = groups[g]
+            if g >= 8:
+                out_pass(g, 0)
+            out_pass(g, 1)
+            staged = sb("y_sb%d" % g, [P, BANK], F32, "page%d" % g if g < 7 else "h2_%d" % (g - 7))
+            if g % 2 == 0:
+                nc.scalar.activation(staged[:], accs[g][:], ACT.Identity, bias=rest_sb[:, c : c + 1])
+            else:
+                nc.vector.tensor_scalar(staged[:], accs[g][:], rest_sb[:, c : c + 1], None, ALU.add)
+            nc.sync.dma_start(out[P * c : P * (c + 1), BANK * half : BANK * (half + 1)], staged[:])

@@ -78,11 +78,11 @@ def tile_list_blendshape_rig_weave_kernel(
             nc.vector.tensor_copy(plane[:], scales[:].indirect(offsets[:]))
             return codes, plane
 
-        def reorder(name, raw, dtype):
+        def reorder(name, raw, dtype, run):
             moved = sb(name, list(raw.shape), raw.dtype)
             nc.vector.tensor_copy(
-                moved[:].bitcast(dtype).rearrange("p (b t m) -> p b m t", b=PASSES, t=PACK),
-                raw[:].bitcast(dtype).rearrange("p (b m t) -> p b m t", b=PASSES, t=PACK),
+                moved[:].bitcast(dtype).rearrange("p (b t m i) -> p b m t i", b=PASSES, t=PACK, i=run),
+                raw[:].bitcast(dtype).rearrange("p (b m i t) -> p b m t i", b=PASSES, t=PACK, i=run),
             )
             return moved
 
@@ -118,7 +118,7 @@ def tile_list_blendshape_rig_weave_kernel(
 
         idx1 = load_list("idx1", offs)
         tab1 = load_bytes("tab1", tab_words[0].rearrange("p t i -> p (t i)"), T, I32)
-        tab1_scales = load_scales("tab1_scales", tab_scales, T, nc.vector, nc.scalar)
+        tab1_scales = load_scales("tab1_scales", tab_scales, T, nc.vector, nc.sync)
         w1_raw = [load_rows("w1_raw0", w1[:, 0:BANK])]
         w2_raw = load_bytes("w2_raw", w2_words[0], 2 * H, U8)
         w2_scales_raw = load_scales("w2_scales_raw", w2_scales, H, nc.vector, nc.gpsimd)
@@ -130,17 +130,17 @@ def tile_list_blendshape_rig_weave_kernel(
         w4_raw = [load_rows("w4_raw%d" % b, w4[:, BANK * b : BANK * (b + 1)]) for b in range(PASSES)]
         idx2 = load_list("idx2", offs2)
         tab2 = load_bytes("tab2", tab2_words[0].rearrange("p t i -> p (t i)"), T, I32)
-        tab2_scales_raw = load_scales("tab2_scales", tab2_scales, T, nc.vector, nc.gpsimd)
+        tab2_scales_raw = load_scales("tab2_scales", tab2_scales, T, nc.vector, nc.sync)
         w3_raw = load_bytes("w3_raw", w3_words[0].rearrange("p c i -> p (c i)"), H, I32)
-        w3_scales_raw = load_scales("w3_scales_raw", w3_scales, H, nc.vector, nc.gpsimd)
+        w3_scales_raw = load_scales("w3_scales_raw", w3_scales, H, nc.vector, nc.sync)
 
         v1 = gather("v1", tab1, tab1_scales, idx1)
         w1_mx = [mx_operand("w1_%d" % b, BANK) for b in range(PASSES)]
-        w1_stage0 = sb("w1_stage0", [P, PACK * BANK], BF16, "tab1_scales")
+        w1_stage0 = sb("w1_stage0", [P, PACK * BANK], BF16, "stage_a")
         cast_reordered(nc.vector.tensor_copy, w1_stage0, w1_raw[0], 0, 1)
-        w2_codes = reorder("w2_codes", w2_raw, U16)
+        w2_codes = reorder("w2_codes", w2_raw, U16, 8)
         quantize(w1_mx[0], w1_stage0, 0, P)
-        w2_plane = reorder("w2_plane", w2_scales_raw, U8)
+        w2_plane = reorder("w2_plane", w2_scales_raw, U8, 16)
         cast_reordered(nc.vector.tensor_copy, w1_stage0, w1_raw[0], 1, PACK)
 
         slot_of = [0, 1, 2, 3, 1, 2, 3, 0]
@@ -183,13 +183,13 @@ def tile_list_blendshape_rig_weave_kernel(
         mouth(1, "act1", "h1")
         mouth(2, "page1", "h2")
         put_mouth(1)
-        w1_stage1 = sb("w1_stage1", [P, PACK * BANK], BF16)
+        w1_stage1 = sb("w1_stage1", [P, PACK * BANK], BF16, "act0")
         cast_reordered(nc.scalar.copy, w1_stage1, w1_raw[1], 0, PACK)
         quantize(w1_mx[1], w1_stage1, 0, BANK)
-        mouth(3, "page2", "w1_stage1")
+        mouth(3, "page2", "act0")
         put_mouth(2)
         audio_mx = mx_operand("audio", S)
-        audio_stage = sb("audio_stage", [P, PACK * S], BF16, "tab1_scales")
+        audio_stage = sb("audio_stage", [P, PACK * S], BF16, "stage_a")
         cast_plain(audio_stage[:], audio_raw)
         quantize(audio_mx, audio_stage, 0, S)
         w4_mx = [mx_operand("w4_%d" % b, BANK) for b in range(PASSES)]
@@ -198,26 +198,26 @@ def tile_list_blendshape_rig_weave_kernel(
             cast_reordered(nc.scalar.copy, stage, w4_raw[b], 0, PACK)
             quantize(w4_mx[b], stage, 0, BANK)
         v2 = gather("v2", tab2, tab2_scales_raw, idx2)
-        w3_plane = reorder("w3_plane", w3_scales_raw, U8)
-        w3_codes = reorder("w3_codes", w3_raw, I32)
-        mouth(4, "page3", "w3_raw")
+        w3_codes = reorder("w3_codes", w3_raw, I32, 4)
+        w3_plane = reorder("w3_plane", w3_scales_raw, U8, 16)
+        mouth(4, "page3", "w4_stage1")
         put_mouth(3)
-        mouth(5, "page4", "h0")
+        mouth(5, "page4", "w3_scales_raw")
         put_mouth(4)
 
+        gain_sb = sb("gain_sb", [P, PASSES, PACK], F32)
+        bias_sb = sb("bias_sb", [P, PASSES, PACK], F32)
+        idx4 = load_list("idx4", offs4)
+        gates2 = load_gates("gates2", wg2, 0, PACK)
+        nc.sync.dma_start(gain_sb[:], gain.rearrange("(b p t) -> p b t", b=PASSES, t=PACK))
+        nc.sync.dma_start(bias_sb[:], bias.rearrange("(b p t) -> p b t", b=PASSES, t=PACK))
         w5_raw = {}
-        free_tags = ["tab1", "w1_raw0", "w1_raw1", None]
+        free_tags = ["tab1", "w1_raw0", "w1_raw1", "audio_raw"]
         for b in range(PASSES):
             for u in range(2):
                 src = w5[BANK * b : BANK * (b + 1), W5_PIECE * u : W5_PIECE * (u + 1)]
                 w5_raw[b, u] = load_rows("w5_raw%d%d" % (b, u), src, free_tags[2 * b + u])
-        gain_sb = sb("gain_sb", [P, PASSES, PACK], F32)
-        bias_sb = sb("bias_sb", [P, PASSES, PACK], F32)
-        nc.sync.dma_start(gain_sb[:], gain.rearrange("(b p t) -> p b t", b=PASSES, t=PACK))
-        nc.sync.dma_start(bias_sb[:], bias.rearrange("(b p t) -> p b t", b=PASSES, t=PACK))
-        idx4 = load_list("idx4", offs4)
-        gates2 = load_gates("gates2", wg2, 0, PACK, "w4_raw1")
-        rest_sb = sb("rest_sb", [P, N_TILES], F32)
+        rest_sb = sb("rest_sb", [P, N_TILES], F32, "tab2")
         with nc.allow_non_contiguous_dma(reason="one value of rest for each partition and tile"):
             nc.sync.dma_start(rest_sb[:], rest.rearrange("(c p) -> p c", p=P))
 
@@ -233,24 +233,31 @@ def tile_list_blendshape_rig_weave_kernel(
             h2[s] = sb("h2_%d" % s, [P, S], F32)
             nc.scalar.activation(h2[s][:], acc[:], ACT.Gelu_apprx_tanh)
 
-        w5_mx = [mx_operand("w5_%d" % b, N) for b in range(PASSES)]
-        for b in range(PASSES):
-            stage = sb("w5_stage%d" % b, [P, PACK * N], BF16)
-            for u in range(2):
-                cast_plain(stage[:, PACK * W5_PIECE * u : PACK * W5_PIECE * (u + 1)], w5_raw[b, u])
-            quantize(w5_mx[b], stage, 0, BANK)
-            quantize(w5_mx[b], stage, BANK, N)
-
         for s in range(SLICES):
             brow(s)
 
-        x_tags = ["tab1_scales", "w4_stage0", None, None]
+        w5_stage = [sb("w5_stage%d" % b, [P, PACK * N], BF16) for b in range(PASSES)]
+        for b in range(PASSES):
+            for u in range(2):
+                cast_plain(w5_stage[b][:, PACK * W5_PIECE * u : PACK * W5_PIECE * (u + 1)], w5_raw[b, u])
+        w5_mx = {}
+
+        def quantize_w5(b, tag):
+            w5_mx[b] = sb("w5_codes%d" % b, [P, N], U32, tag), sb("w5_plane%d" % b, [P, N], U8)
+            quantize(w5_mx[b], w5_stage[b], 0, BANK)
+            quantize(w5_mx[b], w5_stage[b], BANK, N)
+
+        x_tags = ["stage_a", "w4_stage0", None, None]
         x_stage = {}
         x_mx = {}
         for b in range(PASSES):
             for half in range(HALVES):
                 x_stage[b, half] = sb("x_stage%d%d" % (b, half), [P, PACK * BANK], BF16, x_tags[2 * b + half])
-                x_mx[b, half] = mx_operand("x%d%d" % (b, half), BANK)
+
+        def quantize_x(b, half, tag=None):
+            name = "x%d%d" % (b, half)
+            x_mx[b, half] = sb(name + "_codes", [P, BANK], U32, tag), sb(name + "_plane", [P, BANK], U8)
+            quantize(x_mx[b, half], x_stage[b, half], 0, BANK)
 
         def put_brow(s):
             nc.vector.tensor_tensor(pages[s][:].indirect(idx4[:]), h2[s][:], gates2[:, slot_of[s], :], ALU.mult)
@@ -264,6 +271,18 @@ def tile_list_blendshape_rig_weave_kernel(
                 nc.vector.tensor_scalar(dst, src, g, c, ALU.mult, ALU.add)
             else:
                 nc.scalar.activation(dst, src, ACT.Identity, bias=c, scale=g)
+
+        planes = sb("planes", [P, PACK, T2], BF16, "w4_raw0")
+
+        def affine_plane(s):
+            g, c = gain_sb[:, 0, s : s + 1], bias_sb[:, 0, s : s + 1]
+            nc.scalar.activation(planes[:, s, :], pages[s][:], ACT.Identity, bias=c, scale=g)
+
+        def interleave(half):
+            nc.scalar.copy(
+                x_stage[0, half][:].rearrange("p (c i t) -> p c t i", i=4, t=PACK),
+                planes[:, :, BANK * half : BANK * (half + 1)].rearrange("p t (c i) -> p c t i", i=4),
+            )
 
         groups = [(half, c) for half in range(HALVES) for c in range(N_TILES)]
         accs = {}
@@ -281,26 +300,35 @@ def tile_list_blendshape_rig_weave_kernel(
             put_brow(s)
             if s == last - 2:
                 mouth_products(last, "page%d" % PACK)
-            for half in range(HALVES):
-                affine(s, half, False)
+            if s < PACK:
+                affine_plane(s)
+            else:
+                for half in range(HALVES):
+                    affine(s, half, False)
+            if s == 1:
+                quantize_w5(0, "h2_1")
             if s == PACK - 1:
                 for half in range(HALVES):
-                    quantize(x_mx[0, half], x_stage[0, half], 0, BANK)
+                    interleave(half)
+                quantize_x(0, 1)
+            if s == PACK:
+                quantize_w5(1, "h2_4")
+        put_mouth(last)
+        quantize_x(0, 0, "h2_%d" % (last - 2))
         for g in range(8):
             out_pass(g, 0)
-        put_mouth(last)
         put_brow(last)
         affine(last, 0, True)
         affine(last, 1, False)
         for half in range(HALVES):
-            quantize(x_mx[1, half], x_stage[1, half], 0, BANK)
+            quantize_x(1, half)
 
         for g in range(len(groups)):
             half, c = groups[g]
             if g >= 8:
                 out_pass(g, 0)
             out_pass(g, 1)
-            staged = sb("y_sb%d" % g, [P, BANK], F32, "page%d" % g if g < 7 else "h2_%d" % (g - 7))
+            staged = sb("y_sb%d" % g, [P, BANK], F32, "page%d" % g if g < 7 else ["h2_0", "h2_2", "h2_3", "h0", "h1"][g - 7])
             if g % 2 == 0:
                 nc.scalar.activation(staged[:], accs[g][:], ACT.Identity, bias=rest_sb[:, c : c + 1])
             else:

@@ -1,6 +1,7 @@
 from contextlib import ExitStack
 
 import concourse.mybir as mybir
+from concourse.masks import make_identity
 
 T, S, K, H, N, T2 = 2048, 512, 512, 1024, 768, 1024
 FLOPS = 2 * (4 * K * H * S + H * N * T2)
@@ -18,12 +19,27 @@ ALU = mybir.AluOpType
 
 P = 128
 PACK = 4
-PASSES = H // (P * PACK)
-SLICES = PASSES * PACK
+QUADRANT = 32
 BANK = 512
+BANKS = 8
+PASSES = H // BANK
+SLICES = PASSES * PACK
+LAST = SLICES - 1
+CHUNKS = S // P
+LIST_COLUMNS = S // 16
 HALVES = T2 // BANK
 N_TILES = N // P
 W5_PIECE = N // 2
+LINE_BYTES = 16
+LEAD = 2
+RING = 4
+assert LEAD == PACK - 2
+
+BANK_ACT, BANK_LINEAR, BANK_SUM, BANK_BROW = 0, 2, 4, 6
+
+
+def slot_of(s):
+    return (s + s // PACK) % PACK
 
 
 def tile_list_blendshape_rig_weave_kernel(
@@ -36,174 +52,216 @@ def tile_list_blendshape_rig_weave_kernel(
         pool = ctx.enter_context(tc.tile_pool(name="pool", bufs=1))
         psum = ctx.enter_context(tc.psum_pool(name="psum", bufs=1))
 
-        def sb(name, shape, dtype, tag=None):
-            return pool.tile(shape, dtype, name=name, tag=tag or name, align_bytes=64)
+        def sb(name, shape, dtype, buffer=None):
+            return pool.tile(shape, dtype, name=name, tag=buffer or name, align_bytes=64)
 
         def bank(name, index):
             return psum.tile([P, BANK], F32, name=name, tag="bank%d" % index)
 
         def load_list(name, src):
-            tile = lists.tile([P, S // 16], U16, name=name)
+            tile = lists.tile([P, LIST_COLUMNS], U16, name=name)
             nc.sync.dma_start(tile[:], src)
             return tile
 
-        def load_bytes(name, src, width, dtype):
+        def load_words(name, src, width, dtype):
             tile = sb(name, [P, width], dtype)
             nc.sync.dma_start(tile[:].bitcast(I32), src.bitcast(I32))
             return tile
 
-        def load_scales(name, src, width, clear, queue):
+        def load_plane(name, src, width):
             tile = sb(name, [P, width], U8)
-            clear.memset(tile[:].bitcast(I32), 0)
-            for q in range(4):
-                queue.dma_start(tile[32 * q : 32 * q + 4, :].bitcast(I32), src[0, 4 * q : 4 * q + 4, :].bitcast(I32))
+            nc.vector.memset(tile[:].bitcast(I32), 0)
+            for q in range(P // QUADRANT):
+                rows = src[0, PACK * q : PACK * (q + 1), :]
+                nc.sync.dma_start(tile[QUADRANT * q : QUADRANT * q + PACK, :].bitcast(I32), rows.bitcast(I32))
             return tile
 
-        def load_rows(name, src, tag=None):
-            tile = sb(name, [P, PACK, src.shape[1]], F32, tag)
+        def load_rows(name, src, buffer=None):
+            tile = sb(name, [P, PACK, src.shape[1]], F32, buffer)
             nc.sync.dma_start(tile[:], src.rearrange("(p j) c -> p j c", j=PACK))
             return tile
 
-        def load_gates(name, src, t0, t1, tag=None):
-            tile = sb(name, [P, t1 - t0, S], F32, tag)
+        def load_gates(name, src, t0, t1):
+            tile = sb(name, [P, t1 - t0, S], F32)
             rows = src.rearrange("(q t) j -> q t j", t=PACK)[:, t0:t1, :]
-            for quadrant in (0, 2, 1, 3):
-                nc.sync.dma_start(tile[32 * quadrant : 32 * quadrant + 32, :, :], rows)
+            for q in (0, 2, 1, 3):
+                nc.sync.dma_start(tile[QUADRANT * q : QUADRANT * (q + 1), :, :], rows)
             return tile
 
-        def gather(name, words, scales, offsets):
-            codes = sb(name + "_codes", [P, S], U32)
-            plane = sb(name + "_plane", [P, S], U8)
-            nc.vector.tensor_copy(codes[:], words[:].bitcast(U32).indirect(offsets[:]))
-            nc.vector.tensor_copy(plane[:], scales[:].indirect(offsets[:]))
-            return codes, plane
+        def mx_operand(name, width, buffer=None):
+            return sb(name + "_words", [P, width], U32, buffer), sb(name + "_plane", [P, width], U8)
 
-        def reorder(name, raw, dtype, run):
-            moved = sb(name, list(raw.shape), raw.dtype)
+        def gather(name, words, plane, offsets):
+            picked = mx_operand(name, S)
+            nc.vector.tensor_copy(picked[0][:], words[:].bitcast(U32).indirect(offsets[:]))
+            nc.vector.tensor_copy(picked[1][:], plane[:].indirect(offsets[:]))
+            return picked
+
+        def sort_by_slot(name, src, dtype, item_bytes):
+            moved = sb(name, [P, H], dtype)
+            run = LINE_BYTES // item_bytes
             nc.vector.tensor_copy(
-                moved[:].bitcast(dtype).rearrange("p (b t m i) -> p b m t i", b=PASSES, t=PACK, i=run),
-                raw[:].bitcast(dtype).rearrange("p (b m i t) -> p b m t i", b=PASSES, t=PACK, i=run),
+                moved[:].rearrange("p (b t m i) -> p b m t i", b=PASSES, t=PACK, i=run),
+                src[:].rearrange("p (b m i t) -> p b m t i", b=PASSES, t=PACK, i=run),
             )
             return moved
 
-        def cast_reordered(copy, stage, raw, t0, t1):
+        def round_rows(copy, stage, raw):
             copy(
-                stage[:].rearrange("p (t m j) -> p m j t", t=PACK, j=PACK)[:, :, :, t0:t1],
-                raw[:].rearrange("p j (m t) -> p m j t", t=PACK)[:, :, :, t0:t1],
+                stage.rearrange("p (c i j) -> p c j i", i=LINE_BYTES // 4, j=PACK),
+                raw[:].rearrange("p j (c i) -> p c j i", i=LINE_BYTES // 4),
             )
 
-        def cast_plain(stage, raw):
+        def round_rows_by_slot(stage, raw):
             nc.scalar.copy(
-                stage.rearrange("p (c i j) -> p c j i", i=4, j=PACK),
-                raw[:].rearrange("p j (c i) -> p c j i", i=4),
+                stage[:].rearrange("p (t m j) -> p m j t", t=PACK, j=PACK),
+                raw[:].rearrange("p j (m t) -> p m j t", t=PACK),
             )
 
         def quantize(operand, stage, c0, c1):
-            codes, plane = operand
+            words, plane = operand
             nc.vector.quantize_mx(
-                out=codes[:, c0:c1].bitcast(FP8X4), scales=plane[:, c0:c1], in_=stage[:, PACK * c0 : PACK * c1]
+                out=words[:, c0:c1].bitcast(FP8X4), scales=plane[:, c0:c1], in_=stage[:, PACK * c0 : PACK * c1]
             )
 
-        def mx_operand(name, width):
-            return sb(name + "_codes", [P, width], U32), sb(name + "_plane", [P, width], U8)
-
-        def matmul(acc, lhs_codes, lhs_plane, rhs, start, stop):
+        def matmul(acc, lhs, c0, rhs_words, rhs_plane, start, stop):
             nc.tensor.matmul_mx(
-                out=acc[:], lhsT=lhs_codes, lhsT_scale=lhs_plane, rhs=rhs[0][:].bitcast(FP8X4), rhs_scale=rhs[1][:],
-                start=start, stop=stop,
+                out=acc[:], lhsT=lhs[0][:, c0 : c0 + P].bitcast(FP8X4), lhsT_scale=lhs[1][:, c0 : c0 + P],
+                rhs=rhs_words, rhs_scale=rhs_plane, start=start, stop=stop,
             )
 
-        def matmul8(acc, lhs, c0, rhs, start, stop):
-            matmul(acc, lhs[0][:, c0 : c0 + P].bitcast(FP8X4), lhs[1][:, c0 : c0 + P], rhs, start, stop)
+        def matmul_e4m3(acc, lhs, c0, rhs, start, stop):
+            matmul(acc, lhs, c0, rhs[0][:].bitcast(FP8X4), rhs[1][:], start, stop)
 
         idx1 = load_list("idx1", offs)
-        tab1 = load_bytes("tab1", tab_words[0].rearrange("p t i -> p (t i)"), T, I32)
-        tab1_scales = load_scales("tab1_scales", tab_scales, T, nc.vector, nc.sync)
-        w1_raw = [load_rows("w1_raw0", w1[:, 0:BANK])]
-        w2_raw = load_bytes("w2_raw", w2_words[0], 2 * H, U8)
-        w2_scales_raw = load_scales("w2_scales_raw", w2_scales, H, nc.vector, nc.gpsimd)
+        tab1 = load_words("tab1", tab_words[0].rearrange("p t i -> p (t i)"), T, I32)
+        tab1_plane = load_plane("tab1_plane", tab_scales, T)
         idx3 = load_list("idx3", offs3)
-        gates1_first = load_gates("gates1_first", wg1, 0, 1)
-        gates1_rest = load_gates("gates1_rest", wg1, 1, PACK)
-        w1_raw.append(load_rows("w1_raw1", w1[:, BANK:H]))
+        w2_packed = load_words("w2_packed", w2_words[0], 2 * H, U8)
+        piece = BANK // 2
+        w1_pieces = [load_rows("w1_piece%d" % u, w1[:, piece * u : piece * (u + 1)]) for u in range(2)]
+        w2_plane = load_plane("w2_plane", w2_scales, H)
+        gates1_lead = load_gates("gates1_lead", wg1, 0, LEAD)
+        gates1_rest = load_gates("gates1_rest", wg1, LEAD, PACK)
+        w1_raw1 = load_rows("w1_raw1", w1[:, BANK:H])
         audio_raw = load_rows("audio_raw", audio)
         w4_raw = [load_rows("w4_raw%d" % b, w4[:, BANK * b : BANK * (b + 1)]) for b in range(PASSES)]
         idx2 = load_list("idx2", offs2)
-        tab2 = load_bytes("tab2", tab2_words[0].rearrange("p t i -> p (t i)"), T, I32)
-        tab2_scales_raw = load_scales("tab2_scales", tab2_scales, T, nc.vector, nc.sync)
-        w3_raw = load_bytes("w3_raw", w3_words[0].rearrange("p c i -> p (c i)"), H, I32)
-        w3_scales_raw = load_scales("w3_scales_raw", w3_scales, H, nc.vector, nc.sync)
+        tab2 = load_words("tab2", tab2_words[0].rearrange("p t i -> p (t i)"), T, I32)
+        tab2_plane = load_plane("tab2_plane", tab2_scales, T)
+        w3_raw = load_words("w3_raw", w3_words[0].rearrange("p c i -> p (c i)"), H, I32)
+        w3_plane_raw = load_plane("w3_plane_raw", w3_scales, H)
 
-        v1 = gather("v1", tab1, tab1_scales, idx1)
+        identity = sb("identity", [P, P], F32)
+        make_identity(nc, identity[:])
+        v1 = gather("v1", tab1, tab1_plane, idx1)
         w1_mx = [mx_operand("w1_%d" % b, BANK) for b in range(PASSES)]
-        w1_stage0 = sb("w1_stage0", [P, PACK * BANK], BF16, "stage_a")
-        cast_reordered(nc.vector.tensor_copy, w1_stage0, w1_raw[0], 0, 1)
-        w2_codes = reorder("w2_codes", w2_raw, U16, 8)
-        quantize(w1_mx[0], w1_stage0, 0, P)
-        w2_plane = reorder("w2_plane", w2_scales_raw, U8, 16)
-        cast_reordered(nc.vector.tensor_copy, w1_stage0, w1_raw[0], 1, PACK)
+        turned, h1, h2, pages, page_buffer = {}, {}, {}, {}, {}
 
-        slot_of = [0, 1, 2, 3, 1, 2, 3, 0]
-        h1 = {}
-        h2 = {}
-        pages = {}
+        def turned_tiles(b):
+            acts = sb("acts%d" % b, [P, CHUNKS, BANK], F32, "tab1")
+            linear = sb("linear%d" % b, [P, CHUNKS, BANK], F32, "linear")
+            turned[b] = (acts, linear)
 
-        held = {}
+        def mouth_products(b, c, copy):
+            acts, linear = turned[b]
+            acc_b = bank("b%d%d" % (b, c), BANK_LINEAR + c % 2)
+            w2_half = w2_packed[:, 2 * BANK * b : 2 * BANK * (b + 1)].bitcast(FP4X4)
+            matmul(acc_b, v1, P * c, w2_half, w2_plane[:, BANK * b : BANK * (b + 1)], True, True)
+            acc_a = bank("a%d%d" % (b, c), BANK_ACT + c % 2)
+            matmul_e4m3(acc_a, v1, P * c, w1_mx[b], True, True)
+            nc.scalar.activation(
+                acts[:, c, :].rearrange("p (t m) -> p t m", t=PACK),
+                acc_a[:].rearrange("p (m t) -> p t m", t=PACK), ACT.Gelu_apprx_tanh,
+            )
+            copy(
+                linear[:, c, :].rearrange("p (t m) -> p t m", t=PACK),
+                acc_b[:].rearrange("p (m t) -> p t m", t=PACK),
+            )
 
-        def mouth_products(s, gelu_tag):
-            b, t = s // PACK, slot_of[s]
-            acc_a = bank("a%d" % s, 4)
-            acc_b = bank("b%d" % s, [5, 6, 0, 1, 2, 3, 5, 6][s])
-            matmul8(acc_a, w1_mx[b], P * t, v1, True, True)
-            c0 = BANK * b + P * t
-            matmul(acc_b, w2_codes[:, 2 * c0 : 2 * c0 + 2 * P].bitcast(FP4X4), w2_plane[:, c0 : c0 + P], v1, True, True)
-            act = sb("act%d" % s, [P, S], F32, gelu_tag)
-            nc.scalar.activation(act[:], acc_a[:], ACT.Gelu_apprx_tanh)
-            held[s] = (act, acc_b)
+        def mouth_sum(name, index, blocks):
+            acc = bank(name, index)
+            for n, (s, c) in enumerate(blocks):
+                t = slot_of(s)
+                for term, values in enumerate(turned[s // PACK]):
+                    nc.tensor.matmul(
+                        acc[:, P * n : P * (n + 1)], values[:, c, P * t : P * (t + 1)], identity[:],
+                        start=(n == 0 and term == 0), stop=(n == len(blocks) - 1 and term == 1), is_transpose=True,
+                    )
+            return acc
 
-        def mouth_sum(s, h_tag):
-            act, acc_b = held[s]
-            h1[s] = sb("h1_%d" % s, [P, S], F32, h_tag)
-            nc.vector.tensor_tensor(h1[s][:], acc_b[:], act[:], ALU.add)
+        def slice_sum(s):
+            return mouth_sum("sum%d" % s, BANK_SUM + s % 2, [(s, c) for c in range(CHUNKS)])
 
-        def mouth(s, gelu_tag, h_tag):
-            mouth_products(s, gelu_tag)
-            mouth_sum(s, h_tag)
+        def fetch_sum(s, acc, buffer):
+            h1[s] = sb("h1_%d" % s, [P, S], F32, buffer)
+            nc.scalar.copy(h1[s][:], acc[:])
 
-        def put_mouth(s):
-            t = slot_of[s]
-            gate = gates1_first[:, 0, :] if t == 0 else gates1_rest[:, t - 1, :]
-            pages[s] = sb("page%d" % s, [P, T2], F32)
-            nc.vector.tensor_tensor(pages[s][:].indirect(idx3[:]), h1[s][:], gate, ALU.mult)
+        def mouth_slice(s):
+            fetch_sum(s, slice_sum(s), "ring%d" % (s % RING))
 
-        mouth(0, "act0", "h0")
-        quantize(w1_mx[0], w1_stage0, P, 2 * P)
-        quantize(w1_mx[0], w1_stage0, 2 * P, BANK)
-        put_mouth(0)
-        mouth(1, "act1", "h1")
-        mouth(2, "page1", "h2")
-        put_mouth(1)
-        w1_stage1 = sb("w1_stage1", [P, PACK * BANK], BF16, "act0")
-        cast_reordered(nc.scalar.copy, w1_stage1, w1_raw[1], 0, PACK)
+        def gate1(s):
+            t = slot_of(s)
+            return gates1_lead[:, t, :] if t < LEAD else gates1_rest[:, t - LEAD, :]
+
+        def open_page(s, buffer=None):
+            page_buffer[s] = buffer or "page%d" % s
+            pages[s] = sb("page%d" % s, [P, T2], F32, page_buffer[s])
+
+        def put_mouth(s, buffer=None):
+            open_page(s, buffer)
+            nc.vector.tensor_tensor(pages[s][:].indirect(idx3[:]), h1[s][:], gate1(s), ALU.mult)
+
+        def put_lead(c):
+            lead = sb("lead%d" % c, [P, LEAD, P], F32)
+            acc = mouth_sum("lead_sum%d" % c, BANK_BROW + c % 2, [(s, c) for s in range(LEAD)])
+            nc.scalar.copy(lead[:].rearrange("p s j -> p (s j)"), acc[:, 0 : LEAD * P])
+            entries = idx3[:, LIST_COLUMNS // CHUNKS * c : LIST_COLUMNS // CHUNKS * (c + 1)]
+            for s in range(LEAD):
+                window = pages[s][:].indirect(entries)
+                nc.vector.tensor_tensor(window, lead[:, s, :], gate1(s)[:, P * c : P * (c + 1)], ALU.mult)
+
+        w1_stage0 = sb("w1_stage0", [P, PACK * BANK], BF16)
+        for u, copy in enumerate((nc.scalar.copy, nc.vector.tensor_copy)):
+            round_rows(copy, w1_stage0[:, PACK * piece * u : PACK * piece * (u + 1)], w1_pieces[u])
+            quantize(w1_mx[0], w1_stage0, piece * u, piece * (u + 1))
+        turned_tiles(0)
+        for s in range(LEAD):
+            open_page(s)
+        for c in range(CHUNKS):
+            mouth_products(0, c, nc.vector.tensor_copy if c < CHUNKS // 2 else nc.scalar.copy)
+            if c > 0:
+                put_lead(c - 1)
+        put_lead(CHUNKS - 1)
+        for s in range(LEAD, PACK):
+            mouth_slice(s)
+        put_mouth(LEAD)
+
+        after_lead = "lead%d" % (CHUNKS - 2)
+        w1_stage1 = sb("w1_stage1", [P, PACK * BANK], BF16, after_lead)
+        round_rows(nc.scalar.copy, w1_stage1[:], w1_raw1)
         quantize(w1_mx[1], w1_stage1, 0, BANK)
-        mouth(3, "page2", "act0")
-        put_mouth(2)
+        put_mouth(PACK - 1, after_lead)
         audio_mx = mx_operand("audio", S)
-        audio_stage = sb("audio_stage", [P, PACK * S], BF16, "stage_a")
-        cast_plain(audio_stage[:], audio_raw)
+        audio_stage = sb("audio_stage", [P, PACK * S], BF16, "w1_stage0")
+        round_rows(nc.scalar.copy, audio_stage[:], audio_raw)
         quantize(audio_mx, audio_stage, 0, S)
+        turned_tiles(1)
+        for c in range(CHUNKS):
+            mouth_products(1, c, nc.scalar.copy)
+        mouth_slice(PACK)
+        mouth_slice(PACK + 1)
+
         w4_mx = [mx_operand("w4_%d" % b, BANK) for b in range(PASSES)]
         for b in range(PASSES):
-            stage = sb("w4_stage%d" % b, [P, PACK * BANK], BF16)
-            cast_reordered(nc.scalar.copy, stage, w4_raw[b], 0, PACK)
-            quantize(w4_mx[b], stage, 0, BANK)
-        v2 = gather("v2", tab2, tab2_scales_raw, idx2)
-        w3_codes = reorder("w3_codes", w3_raw, I32, 4)
-        w3_plane = reorder("w3_plane", w3_scales_raw, U8, 16)
-        mouth(4, "page3", "w4_stage1")
-        put_mouth(3)
-        mouth(5, "page4", "w3_scales_raw")
-        put_mouth(4)
+            w4_stage = sb("w4_stage%d" % b, [P, PACK * BANK], BF16)
+            round_rows_by_slot(w4_stage, w4_raw[b])
+            quantize(w4_mx[b], w4_stage, 0, BANK)
+        v2 = gather("v2", tab2, tab2_plane, idx2)
+        w3_mx = (sort_by_slot("w3_sorted", w3_raw, I32, 4), sort_by_slot("w3_plane", w3_plane_raw, U8, 1))
+        put_mouth(PACK, "w3_plane_raw")
+        mouth_slice(LAST - 1)
+        last_sum = slice_sum(LAST)
 
         gain_sb = sb("gain_sb", [P, PASSES, PACK], F32)
         bias_sb = sb("bias_sb", [P, PASSES, PACK], F32)
@@ -212,125 +270,120 @@ def tile_list_blendshape_rig_weave_kernel(
         nc.sync.dma_start(gain_sb[:], gain.rearrange("(b p t) -> p b t", b=PASSES, t=PACK))
         nc.sync.dma_start(bias_sb[:], bias.rearrange("(b p t) -> p b t", b=PASSES, t=PACK))
         w5_raw = {}
-        free_tags = ["tab1", "w1_raw0", "w1_raw1", "audio_raw"]
+        used_up = ["w1_piece0", "w1_raw1", "audio_raw", "tab1"]
         for b in range(PASSES):
             for u in range(2):
                 src = w5[BANK * b : BANK * (b + 1), W5_PIECE * u : W5_PIECE * (u + 1)]
-                w5_raw[b, u] = load_rows("w5_raw%d%d" % (b, u), src, free_tags[2 * b + u])
+                w5_raw[b, u] = load_rows("w5_raw%d%d" % (b, u), src, used_up[2 * b + u])
         rest_sb = sb("rest_sb", [P, N_TILES], F32, "tab2")
-        with nc.allow_non_contiguous_dma(reason="one value of rest for each partition and tile"):
+        with nc.allow_non_contiguous_dma(reason="one value of rest for each partition and tile of out"):
             nc.sync.dma_start(rest_sb[:], rest.rearrange("(c p) -> p c", p=P))
 
-        mouth(6, "page5", "h1")
-        put_mouth(5)
-        put_mouth(6)
-
-        def brow(s):
-            b, t = s // PACK, slot_of[s]
-            acc = bank("e%d" % s, 7 * (s % 2))
-            matmul8(acc, (w3_codes, w3_plane), BANK * b + P * t, v2, True, False)
-            matmul8(acc, w4_mx[b], P * t, audio_mx, False, True)
-            h2[s] = sb("h2_%d" % s, [P, S], F32)
-            nc.scalar.activation(h2[s][:], acc[:], ACT.Gelu_apprx_tanh)
+        put_mouth(PACK + 1, "w4_stage1")
 
         for s in range(SLICES):
-            brow(s)
+            b, t = s // PACK, slot_of(s)
+            acc = bank("e%d" % s, BANK_BROW + s % 2)
+            matmul_e4m3(acc, w3_mx, BANK * b + P * t, v2, True, False)
+            matmul_e4m3(acc, w4_mx[b], P * t, audio_mx, False, True)
+            h2[s] = sb("h2_%d" % s, [P, S], F32)
+            nc.scalar.activation(h2[s][:], acc[:], ACT.Gelu_apprx_tanh)
 
         w5_stage = [sb("w5_stage%d" % b, [P, PACK * N], BF16) for b in range(PASSES)]
         for b in range(PASSES):
             for u in range(2):
-                cast_plain(w5_stage[b][:, PACK * W5_PIECE * u : PACK * W5_PIECE * (u + 1)], w5_raw[b, u])
-        w5_mx = {}
+                columns = slice(PACK * W5_PIECE * u, PACK * W5_PIECE * (u + 1))
+                round_rows(nc.scalar.copy, w5_stage[b][:, columns], w5_raw[b, u])
 
-        def quantize_w5(b, tag):
-            w5_mx[b] = sb("w5_codes%d" % b, [P, N], U32, tag), sb("w5_plane%d" % b, [P, N], U8)
+        w5_mx, x_mx, x_stage, sums = {}, {}, {}, {}
+        idle_stages = {(0, 0): "w1_stage0", (0, 1): "w4_stage0"}
+        for b in range(PASSES):
+            for half in range(HALVES):
+                x_stage[b, half] = sb("x_stage%d%d" % (b, half), [P, PACK * BANK], BF16, idle_stages.get((b, half)))
+        x_rows = sb("x_rows", [P, PACK, T2], BF16, "w4_raw0")
+
+        def quantize_w5(b, buffer):
+            w5_mx[b] = mx_operand("w5_%d" % b, N, buffer)
             quantize(w5_mx[b], w5_stage[b], 0, BANK)
             quantize(w5_mx[b], w5_stage[b], BANK, N)
 
-        x_tags = ["stage_a", "w4_stage0", None, None]
-        x_stage = {}
-        x_mx = {}
-        for b in range(PASSES):
-            for half in range(HALVES):
-                x_stage[b, half] = sb("x_stage%d%d" % (b, half), [P, PACK * BANK], BF16, x_tags[2 * b + half])
-
-        def quantize_x(b, half, tag=None):
-            name = "x%d%d" % (b, half)
-            x_mx[b, half] = sb(name + "_codes", [P, BANK], U32, tag), sb(name + "_plane", [P, BANK], U8)
+        def quantize_x(b, half, buffer=None):
+            x_mx[b, half] = mx_operand("x%d%d" % (b, half), BANK, buffer)
             quantize(x_mx[b, half], x_stage[b, half], 0, BANK)
 
         def put_brow(s):
-            nc.vector.tensor_tensor(pages[s][:].indirect(idx4[:]), h2[s][:], gates2[:, slot_of[s], :], ALU.mult)
+            nc.vector.tensor_tensor(pages[s][:].indirect(idx4[:]), h2[s][:], gates2[:, slot_of(s), :], ALU.mult)
 
-        def affine(s, half, on_vector):
-            b, t = s // PACK, slot_of[s]
-            dst = x_stage[b, half][:].rearrange("p (m t) -> p m t", t=PACK)[:, :, t]
+        def gain_and_bias(s):
+            b, t = s // PACK, slot_of(s)
+            return gain_sb[:, b, t : t + 1], bias_sb[:, b, t : t + 1]
+
+        def affine_row(s):
+            g, c = gain_and_bias(s)
+            nc.scalar.activation(x_rows[:, slot_of(s), :], pages[s][:], ACT.Identity, bias=c, scale=g)
+
+        def interleave(half):
+            nc.scalar.copy(
+                x_stage[0, half][:].rearrange("p (c i t) -> p c t i", i=PACK, t=PACK),
+                x_rows[:, :, BANK * half : BANK * (half + 1)].rearrange("p t (c i) -> p c t i", i=PACK),
+            )
+
+        def affine_in_place(s, half, on_vector=False):
+            g, c = gain_and_bias(s)
+            dst = x_stage[1, half][:].rearrange("p (m t) -> p m t", t=PACK)[:, :, slot_of(s)]
             src = pages[s][:, BANK * half : BANK * (half + 1)]
-            g, c = gain_sb[:, b, t : t + 1], bias_sb[:, b, t : t + 1]
             if on_vector:
                 nc.vector.tensor_scalar(dst, src, g, c, ALU.mult, ALU.add)
             else:
                 nc.scalar.activation(dst, src, ACT.Identity, bias=c, scale=g)
 
-        planes = sb("planes", [P, PACK, T2], BF16, "w4_raw0")
-
-        def affine_plane(s):
-            g, c = gain_sb[:, 0, s : s + 1], bias_sb[:, 0, s : s + 1]
-            nc.scalar.activation(planes[:, s, :], pages[s][:], ACT.Identity, bias=c, scale=g)
-
-        def interleave(half):
-            nc.scalar.copy(
-                x_stage[0, half][:].rearrange("p (c i t) -> p c t i", i=4, t=PACK),
-                planes[:, :, BANK * half : BANK * (half + 1)].rearrange("p t (c i) -> p c t i", i=4),
-            )
-
         groups = [(half, c) for half in range(HALVES) for c in range(N_TILES)]
-        accs = {}
 
         def out_pass(g, b):
             half, c = groups[g]
             if b == 0:
-                accs[g] = bank("y%d" % g, g % 8)
-            matmul8(accs[g], w5_mx[b], P * c, x_mx[b, half], b == 0, b == PASSES - 1)
+                sums[g] = bank("y%d" % g, g % BANKS)
+            matmul_e4m3(sums[g], w5_mx[b], P * c, x_mx[b, half], b == 0, b == PASSES - 1)
 
-        last = SLICES - 1
-        for s in range(last):
-            if s == last - 1:
-                mouth_sum(last, "h2_%d" % (last - 2))
+        for s in range(PACK):
             put_brow(s)
-            if s == last - 2:
-                mouth_products(last, "page%d" % PACK)
-            if s < PACK:
-                affine_plane(s)
-            else:
-                for half in range(HALVES):
-                    affine(s, half, False)
-            if s == 1:
-                quantize_w5(0, "h2_1")
             if s == PACK - 1:
-                for half in range(HALVES):
-                    interleave(half)
-                quantize_x(0, 1)
+                put_mouth(LAST - 1, "h2_%d" % s)
+            affine_row(s)
+            if s == 1:
+                quantize_w5(0, "h2_%d" % s)
+        for half in range(HALVES):
+            interleave(half)
+        quantize_x(0, 1)
+
+        for s in range(PACK, LAST):
+            put_brow(s)
+            if s == PACK + 1:
+                fetch_sum(LAST, last_sum, page_buffer[PACK])
+            for half in range(HALVES):
+                affine_in_place(s, half)
             if s == PACK:
-                quantize_w5(1, "h2_4")
-        put_mouth(last)
-        quantize_x(0, 0, "h2_%d" % (last - 2))
-        for g in range(8):
+                quantize_w5(1, "h2_%d" % s)
+        put_mouth(LAST)
+
+        quantize_x(0, 0, page_buffer[PACK])
+        for g in range(BANKS):
             out_pass(g, 0)
-        put_brow(last)
-        affine(last, 0, True)
-        affine(last, 1, False)
+        put_brow(LAST)
+        affine_in_place(LAST, 0, on_vector=True)
+        affine_in_place(LAST, 1)
         for half in range(HALVES):
             quantize_x(1, half)
 
-        for g in range(len(groups)):
-            half, c = groups[g]
-            if g >= 8:
+        staging = [page_buffer[s] for s in range(LAST) if s != PACK] + ["h2_0", "h2_2"]
+        staging = staging + ["ring%d" % ((n - 1) % RING) for n in range(RING)]
+        for g, (half, c) in enumerate(groups):
+            if g >= BANKS:
                 out_pass(g, 0)
             out_pass(g, 1)
-            staged = sb("y_sb%d" % g, [P, BANK], F32, "page%d" % g if g < 7 else ["h2_0", "h2_2", "h2_3", "h0", "h1"][g - 7])
+            staged = sb("y_sb%d" % g, [P, BANK], F32, staging[g])
             if g % 2 == 0:
-                nc.scalar.activation(staged[:], accs[g][:], ACT.Identity, bias=rest_sb[:, c : c + 1])
+                nc.scalar.activation(staged[:], sums[g][:], ACT.Identity, bias=rest_sb[:, c : c + 1])
             else:
-                nc.vector.tensor_scalar(staged[:], accs[g][:], rest_sb[:, c : c + 1], None, ALU.add)
+                nc.vector.tensor_scalar(staged[:], sums[g][:], rest_sb[:, c : c + 1], None, ALU.add)
             nc.sync.dma_start(out[P * c : P * (c + 1), BANK * half : BANK * (half + 1)], staged[:])

from contextlib import ExitStack

import concourse.mybir as mybir
from concourse.masks import make_identity

T, S, K, H, N, T2 = 2048, 512, 512, 1024, 768, 1024
FLOPS = 2 * (4 * K * H * S + H * N * T2)

F32 = mybir.dt.float32
BF16 = mybir.dt.bfloat16
I32 = mybir.dt.int32
U32 = mybir.dt.uint32
U16 = mybir.dt.uint16
U8 = mybir.dt.uint8
FP8X4 = mybir.dt.float8_e4m3fn_x4
FP4X4 = mybir.dt.float4_e2m1fn_x4
ACT = mybir.ActivationFunctionType
ALU = mybir.AluOpType

P = 128
PACK = 4
QUADRANT = 32
BANK = 512
BANKS = 8
PASSES = H // BANK
SLICES = PASSES * PACK
LAST = SLICES - 1
CHUNKS = S // P
LIST_COLUMNS = S // 16
HALVES = T2 // BANK
N_TILES = N // P
W5_PIECE = N // 2
LINE_BYTES = 16
LEAD = 2
RING = 4
assert LEAD == PACK - 2

BANK_ACT, BANK_LINEAR, BANK_SUM, BANK_BROW = 0, 2, 4, 6


def slot_of(s):
    return (s + s // PACK) % PACK


def tile_list_blendshape_rig_weave_kernel(
    tc, tab_words, tab_scales, tab2_words, tab2_scales, offs, offs2, offs3, offs4, w1, w2_words, w2_scales,
    w3_words, w3_scales, w4, audio, wg1, wg2, gain, bias, w5, rest, out,
):
    nc = tc.nc
    with ExitStack() as ctx:
        lists = ctx.enter_context(tc.tile_pool(name="lists", bufs=1))
        pool = ctx.enter_context(tc.tile_pool(name="pool", bufs=1))
        psum = ctx.enter_context(tc.psum_pool(name="psum", bufs=1))

        def sb(name, shape, dtype, buffer=None):
            return pool.tile(shape, dtype, name=name, tag=buffer or name, align_bytes=64)

        def bank(name, index):
            return psum.tile([P, BANK], F32, name=name, tag="bank%d" % index)

        def load_list(name, src):
            tile = lists.tile([P, LIST_COLUMNS], U16, name=name)
            nc.sync.dma_start(tile[:], src)
            return tile

        def load_words(name, src, width, dtype):
            tile = sb(name, [P, width], dtype)
            nc.sync.dma_start(tile[:].bitcast(I32), src.bitcast(I32))
            return tile

        def load_plane(name, src, width):
            tile = sb(name, [P, width], U8)
            nc.vector.memset(tile[:].bitcast(I32), 0)
            for q in range(P // QUADRANT):
                rows = src[0, PACK * q : PACK * (q + 1), :]
                nc.sync.dma_start(tile[QUADRANT * q : QUADRANT * q + PACK, :].bitcast(I32), rows.bitcast(I32))
            return tile

        def load_rows(name, src, buffer=None):
            tile = sb(name, [P, PACK, src.shape[1]], F32, buffer)
            nc.sync.dma_start(tile[:], src.rearrange("(p j) c -> p j c", j=PACK))
            return tile

        def load_gates(name, src, t0, t1):
            tile = sb(name, [P, t1 - t0, S], F32)
            rows = src.rearrange("(q t) j -> q t j", t=PACK)[:, t0:t1, :]
            for q in (0, 2, 1, 3):
                nc.sync.dma_start(tile[QUADRANT * q : QUADRANT * (q + 1), :, :], rows)
            return tile

        def mx_operand(name, width, buffer=None):
            return sb(name + "_words", [P, width], U32, buffer), sb(name + "_plane", [P, width], U8)

        def gather(name, words, plane, offsets):
            picked = mx_operand(name, S)
            nc.vector.tensor_copy(picked[0][:], words[:].bitcast(U32).indirect(offsets[:]))
            nc.vector.tensor_copy(picked[1][:], plane[:].indirect(offsets[:]))
            return picked

        def sort_by_slot(name, src, dtype, item_bytes):
            moved = sb(name, [P, H], dtype)
            run = LINE_BYTES // item_bytes
            nc.vector.tensor_copy(
                moved[:].rearrange("p (b t m i) -> p b m t i", b=PASSES, t=PACK, i=run),
                src[:].rearrange("p (b m i t) -> p b m t i", b=PASSES, t=PACK, i=run),
            )
            return moved

        def round_rows(copy, stage, raw):
            copy(
                stage.rearrange("p (c i j) -> p c j i", i=LINE_BYTES // 4, j=PACK),
                raw[:].rearrange("p j (c i) -> p c j i", i=LINE_BYTES // 4),
            )

        def round_rows_by_slot(stage, raw):
            nc.scalar.copy(
                stage[:].rearrange("p (t m j) -> p m j t", t=PACK, j=PACK),
                raw[:].rearrange("p j (m t) -> p m j t", t=PACK),
            )

        def quantize(operand, stage, c0, c1):
            words, plane = operand
            nc.vector.quantize_mx(
                out=words[:, c0:c1].bitcast(FP8X4), scales=plane[:, c0:c1], in_=stage[:, PACK * c0 : PACK * c1]
            )

        def matmul(acc, lhs, c0, rhs_words, rhs_plane, start, stop):
            nc.tensor.matmul_mx(
                out=acc[:], lhsT=lhs[0][:, c0 : c0 + P].bitcast(FP8X4), lhsT_scale=lhs[1][:, c0 : c0 + P],
                rhs=rhs_words, rhs_scale=rhs_plane, start=start, stop=stop,
            )

        def matmul_e4m3(acc, lhs, c0, rhs, start, stop):
            matmul(acc, lhs, c0, rhs[0][:].bitcast(FP8X4), rhs[1][:], start, stop)

        idx1 = load_list("idx1", offs)
        tab1 = load_words("tab1", tab_words[0].rearrange("p t i -> p (t i)"), T, I32)
        tab1_plane = load_plane("tab1_plane", tab_scales, T)
        idx3 = load_list("idx3", offs3)
        w2_packed = load_words("w2_packed", w2_words[0], 2 * H, U8)
        piece = BANK // 2
        w1_pieces = [load_rows("w1_piece%d" % u, w1[:, piece * u : piece * (u + 1)]) for u in range(2)]
        w2_plane = load_plane("w2_plane", w2_scales, H)
        gates1_lead = load_gates("gates1_lead", wg1, 0, LEAD)
        gates1_rest = load_gates("gates1_rest", wg1, LEAD, PACK)
        w1_raw1 = load_rows("w1_raw1", w1[:, BANK:H])
        audio_raw = load_rows("audio_raw", audio)
        w4_raw = [load_rows("w4_raw%d" % b, w4[:, BANK * b : BANK * (b + 1)]) for b in range(PASSES)]
        idx2 = load_list("idx2", offs2)
        tab2 = load_words("tab2", tab2_words[0].rearrange("p t i -> p (t i)"), T, I32)
        tab2_plane = load_plane("tab2_plane", tab2_scales, T)
        w3_raw = load_words("w3_raw", w3_words[0].rearrange("p c i -> p (c i)"), H, I32)
        w3_plane_raw = load_plane("w3_plane_raw", w3_scales, H)

        identity = sb("identity", [P, P], F32)
        make_identity(nc, identity[:])
        v1 = gather("v1", tab1, tab1_plane, idx1)
        w1_mx = [mx_operand("w1_%d" % b, BANK) for b in range(PASSES)]
        turned, h1, h2, pages, page_buffer = {}, {}, {}, {}, {}

        def turned_tiles(b):
            acts = sb("acts%d" % b, [P, CHUNKS, BANK], F32, "tab1")
            linear = sb("linear%d" % b, [P, CHUNKS, BANK], F32, "linear")
            turned[b] = (acts, linear)

        def mouth_products(b, c, copy):
            acts, linear = turned[b]
            acc_b = bank("b%d%d" % (b, c), BANK_LINEAR + c % 2)
            w2_half = w2_packed[:, 2 * BANK * b : 2 * BANK * (b + 1)].bitcast(FP4X4)
            matmul(acc_b, v1, P * c, w2_half, w2_plane[:, BANK * b : BANK * (b + 1)], True, True)
            acc_a = bank("a%d%d" % (b, c), BANK_ACT + c % 2)
            matmul_e4m3(acc_a, v1, P * c, w1_mx[b], True, True)
            nc.scalar.activation(
                acts[:, c, :].rearrange("p (t m) -> p t m", t=PACK),
                acc_a[:].rearrange("p (m t) -> p t m", t=PACK), ACT.Gelu_apprx_tanh,
            )
            copy(
                linear[:, c, :].rearrange("p (t m) -> p t m", t=PACK),
                acc_b[:].rearrange("p (m t) -> p t m", t=PACK),
            )

        def mouth_sum(name, index, blocks):
            acc = bank(name, index)
            for n, (s, c) in enumerate(blocks):
                t = slot_of(s)
                for term, values in enumerate(turned[s // PACK]):
                    nc.tensor.matmul(
                        acc[:, P * n : P * (n + 1)], values[:, c, P * t : P * (t + 1)], identity[:],
                        start=(n == 0 and term == 0), stop=(n == len(blocks) - 1 and term == 1), is_transpose=True,
                    )
            return acc

        def slice_sum(s):
            return mouth_sum("sum%d" % s, BANK_SUM + s % 2, [(s, c) for c in range(CHUNKS)])

        def fetch_sum(s, acc, buffer):
            h1[s] = sb("h1_%d" % s, [P, S], F32, buffer)
            nc.scalar.copy(h1[s][:], acc[:])

        def mouth_slice(s):
            fetch_sum(s, slice_sum(s), "ring%d" % (s % RING))

        def gate1(s):
            t = slot_of(s)
            return gates1_lead[:, t, :] if t < LEAD else gates1_rest[:, t - LEAD, :]

        def open_page(s, buffer=None):
            page_buffer[s] = buffer or "page%d" % s
            pages[s] = sb("page%d" % s, [P, T2], F32, page_buffer[s])

        def put_mouth(s, buffer=None):
            open_page(s, buffer)
            nc.vector.tensor_tensor(pages[s][:].indirect(idx3[:]), h1[s][:], gate1(s), ALU.mult)

        def put_lead(c):
            lead = sb("lead%d" % c, [P, LEAD, P], F32)
            acc = mouth_sum("lead_sum%d" % c, BANK_BROW + c % 2, [(s, c) for s in range(LEAD)])
            nc.scalar.copy(lead[:].rearrange("p s j -> p (s j)"), acc[:, 0 : LEAD * P])
            entries = idx3[:, LIST_COLUMNS // CHUNKS * c : LIST_COLUMNS // CHUNKS * (c + 1)]
            for s in range(LEAD):
                window = pages[s][:].indirect(entries)
                nc.vector.tensor_tensor(window, lead[:, s, :], gate1(s)[:, P * c : P * (c + 1)], ALU.mult)

        w1_stage0 = sb("w1_stage0", [P, PACK * BANK], BF16)
        for u, copy in enumerate((nc.scalar.copy, nc.vector.tensor_copy)):
            round_rows(copy, w1_stage0[:, PACK * piece * u : PACK * piece * (u + 1)], w1_pieces[u])
            quantize(w1_mx[0], w1_stage0, piece * u, piece * (u + 1))
        turned_tiles(0)
        for s in range(LEAD):
            open_page(s)
        for c in range(CHUNKS):
            mouth_products(0, c, nc.vector.tensor_copy if c < CHUNKS // 2 else nc.scalar.copy)
            if c > 0:
                put_lead(c - 1)
        put_lead(CHUNKS - 1)
        for s in range(LEAD, PACK):
            mouth_slice(s)
        put_mouth(LEAD)

        after_lead = "lead%d" % (CHUNKS - 2)
        w1_stage1 = sb("w1_stage1", [P, PACK * BANK], BF16, after_lead)
        round_rows(nc.scalar.copy, w1_stage1[:], w1_raw1)
        quantize(w1_mx[1], w1_stage1, 0, BANK)
        put_mouth(PACK - 1, after_lead)
        audio_mx = mx_operand("audio", S)
        audio_stage = sb("audio_stage", [P, PACK * S], BF16, "w1_stage0")
        round_rows(nc.scalar.copy, audio_stage[:], audio_raw)
        quantize(audio_mx, audio_stage, 0, S)
        turned_tiles(1)
        for c in range(CHUNKS):
            mouth_products(1, c, nc.scalar.copy)
        mouth_slice(PACK)
        mouth_slice(PACK + 1)

        w4_mx = [mx_operand("w4_%d" % b, BANK) for b in range(PASSES)]
        for b in range(PASSES):
            w4_stage = sb("w4_stage%d" % b, [P, PACK * BANK], BF16)
            round_rows_by_slot(w4_stage, w4_raw[b])
            quantize(w4_mx[b], w4_stage, 0, BANK)
        v2 = gather("v2", tab2, tab2_plane, idx2)
        w3_mx = (sort_by_slot("w3_sorted", w3_raw, I32, 4), sort_by_slot("w3_plane", w3_plane_raw, U8, 1))
        put_mouth(PACK, "w3_plane_raw")
        mouth_slice(LAST - 1)
        last_sum = slice_sum(LAST)

        gain_sb = sb("gain_sb", [P, PASSES, PACK], F32)
        bias_sb = sb("bias_sb", [P, PASSES, PACK], F32)
        idx4 = load_list("idx4", offs4)
        gates2 = load_gates("gates2", wg2, 0, PACK)
        nc.sync.dma_start(gain_sb[:], gain.rearrange("(b p t) -> p b t", b=PASSES, t=PACK))
        nc.sync.dma_start(bias_sb[:], bias.rearrange("(b p t) -> p b t", b=PASSES, t=PACK))
        w5_raw = {}
        used_up = ["w1_piece0", "w1_raw1", "audio_raw", "tab1"]
        for b in range(PASSES):
            for u in range(2):
                src = w5[BANK * b : BANK * (b + 1), W5_PIECE * u : W5_PIECE * (u + 1)]
                w5_raw[b, u] = load_rows("w5_raw%d%d" % (b, u), src, used_up[2 * b + u])
        rest_sb = sb("rest_sb", [P, N_TILES], F32, "tab2")
        with nc.allow_non_contiguous_dma(reason="one value of rest for each partition and tile of out"):
            nc.sync.dma_start(rest_sb[:], rest.rearrange("(c p) -> p c", p=P))

        put_mouth(PACK + 1, "w4_stage1")

        for s in range(SLICES):
            b, t = s // PACK, slot_of(s)
            acc = bank("e%d" % s, BANK_BROW + s % 2)
            matmul_e4m3(acc, w3_mx, BANK * b + P * t, v2, True, False)
            matmul_e4m3(acc, w4_mx[b], P * t, audio_mx, False, True)
            h2[s] = sb("h2_%d" % s, [P, S], F32)
            nc.scalar.activation(h2[s][:], acc[:], ACT.Gelu_apprx_tanh)

        w5_stage = [sb("w5_stage%d" % b, [P, PACK * N], BF16) for b in range(PASSES)]
        for b in range(PASSES):
            for u in range(2):
                columns = slice(PACK * W5_PIECE * u, PACK * W5_PIECE * (u + 1))
                round_rows(nc.scalar.copy, w5_stage[b][:, columns], w5_raw[b, u])

        w5_mx, x_mx, x_stage, sums = {}, {}, {}, {}
        idle_stages = {(0, 0): "w1_stage0", (0, 1): "w4_stage0"}
        for b in range(PASSES):
            for half in range(HALVES):
                x_stage[b, half] = sb("x_stage%d%d" % (b, half), [P, PACK * BANK], BF16, idle_stages.get((b, half)))
        x_rows = sb("x_rows", [P, PACK, T2], BF16, "w4_raw0")

        def quantize_w5(b, buffer):
            w5_mx[b] = mx_operand("w5_%d" % b, N, buffer)
            quantize(w5_mx[b], w5_stage[b], 0, BANK)
            quantize(w5_mx[b], w5_stage[b], BANK, N)

        def quantize_x(b, half, buffer=None):
            x_mx[b, half] = mx_operand("x%d%d" % (b, half), BANK, buffer)
            quantize(x_mx[b, half], x_stage[b, half], 0, BANK)

        def put_brow(s):
            nc.vector.tensor_tensor(pages[s][:].indirect(idx4[:]), h2[s][:], gates2[:, slot_of(s), :], ALU.mult)

        def gain_and_bias(s):
            b, t = s // PACK, slot_of(s)
            return gain_sb[:, b, t : t + 1], bias_sb[:, b, t : t + 1]

        def affine_row(s):
            g, c = gain_and_bias(s)
            nc.scalar.activation(x_rows[:, slot_of(s), :], pages[s][:], ACT.Identity, bias=c, scale=g)

        def interleave(half):
            nc.scalar.copy(
                x_stage[0, half][:].rearrange("p (c i t) -> p c t i", i=PACK, t=PACK),
                x_rows[:, :, BANK * half : BANK * (half + 1)].rearrange("p t (c i) -> p c t i", i=PACK),
            )

        def affine_in_place(s, half, on_vector=False):
            g, c = gain_and_bias(s)
            dst = x_stage[1, half][:].rearrange("p (m t) -> p m t", t=PACK)[:, :, slot_of(s)]
            src = pages[s][:, BANK * half : BANK * (half + 1)]
            if on_vector:
                nc.vector.tensor_scalar(dst, src, g, c, ALU.mult, ALU.add)
            else:
                nc.scalar.activation(dst, src, ACT.Identity, bias=c, scale=g)

        groups = [(half, c) for half in range(HALVES) for c in range(N_TILES)]

        def out_pass(g, b):
            half, c = groups[g]
            if b == 0:
                sums[g] = bank("y%d" % g, g % BANKS)
            matmul_e4m3(sums[g], w5_mx[b], P * c, x_mx[b, half], b == 0, b == PASSES - 1)

        for s in range(PACK):
            put_brow(s)
            if s == PACK - 1:
                put_mouth(LAST - 1, "h2_%d" % s)
            affine_row(s)
            if s == 1:
                quantize_w5(0, "h2_%d" % s)
        for half in range(HALVES):
            interleave(half)
        quantize_x(0, 1)

        for s in range(PACK, LAST):
            put_brow(s)
            if s == PACK + 1:
                fetch_sum(LAST, last_sum, page_buffer[PACK])
            for half in range(HALVES):
                affine_in_place(s, half)
            if s == PACK:
                quantize_w5(1, "h2_%d" % s)
        put_mouth(LAST)

        quantize_x(0, 0, page_buffer[PACK])
        for g in range(BANKS):
            out_pass(g, 0)
        put_brow(LAST)
        affine_in_place(LAST, 0, on_vector=True)
        affine_in_place(LAST, 1)
        for half in range(HALVES):
            quantize_x(1, half)

        staging = [page_buffer[s] for s in range(LAST) if s != PACK] + ["h2_0", "h2_2"]
        staging = staging + ["ring%d" % ((n - 1) % RING) for n in range(RING)]
        for g, (half, c) in enumerate(groups):
            if g >= BANKS:
                out_pass(g, 0)
            out_pass(g, 1)
            staged = sb("y_sb%d" % g, [P, BANK], F32, staging[g])
            if g % 2 == 0:
                nc.scalar.activation(staged[:], sums[g][:], ACT.Identity, bias=rest_sb[:, c : c + 1])
            else:
                nc.vector.tensor_scalar(staged[:], sums[g][:], rest_sb[:, c : c + 1], None, ALU.add)
            nc.sync.dma_start(out[P * c : P * (c + 1), BANK * half : BANK * (half + 1)], staged[:])
